import numpy as np
import ml_dtypes


def mxq(x, axis, fmt="e4m3"):
    dtype, down = {"e4m3": (ml_dtypes.float8_e4m3fn, 7), "e5m2": (ml_dtypes.float8_e5m2, 14)}[fmt]
    v = np.moveaxis(np.asarray(x, np.float32).astype(ml_dtypes.bfloat16).astype(np.float64), axis, -1)
    blocks = v.reshape(v.shape[:-1] + (-1, 32))
    amax = np.abs(blocks).max(-1, keepdims=True)
    byte = np.maximum(np.where(amax > 0, np.frexp(amax)[1] - 1 + 127, 0) - down, 1)
    scale = np.exp2(byte - 127.0)
    codes = (blocks / scale).astype(np.float32).astype(dtype).astype(np.float64)
    return np.moveaxis((codes * scale).reshape(v.shape), -1, axis)


WIDE = False


def mx_kscale(k):
    if not WIDE:
        return np.ones(k)
    levels = np.array([30, -30])
    if k % 512:
        return np.exp2(np.random.permutation(np.resize(levels, k // 32))).repeat(32)
    a = np.empty((k // 512, 16))
    for p in range(k // 512):
        a[p, :8] = np.random.permutation(np.resize(levels, 8))
        for g in range(8):
            far = levels[np.abs(levels - a[p, g]) >= 10]
            a[p, g + 8] = far[np.random.randint(len(far))]
    return np.exp2(a.ravel()).repeat(32)


BF16 = ml_dtypes.bfloat16


def bf(x):
    return np.asarray(x, np.float32).astype(BF16)


def f64(x):
    return np.asarray(x).astype(np.float64)


C, F = 1024, 2048


def setup_inputs():
    s, u = mx_kscale(F), mx_kscale(F)
    tail = np.exp(0.6 * np.random.standard_normal((F, C)))
    return {"z": bf(np.random.standard_normal((C, F)) / np.sqrt(F) * s),
            "a_fc": bf(0.7 * np.random.standard_normal((F, C)) * tail / s[:, None]),
            "d": bf((0.75 + 0.1 * np.random.standard_normal(F)) * u / s),
            "w": bf(np.random.standard_normal((F, C)) / u[:, None]),
            "a_cf": bf(np.random.standard_normal((C, F)) / np.sqrt(F) * u),
            "a_cc": bf(np.random.standard_normal((C, C))),
            "tau": bf(3.0 + 0.5 * np.random.standard_normal(C))}


def reference(z, a_fc, d, w, a_cf, a_cc, tau):
    e = f64(d)[:, None] * f64(w) + f64(a_fc)
    coarse = ((mxq(f64(z), 1, "e4m3") @ mxq(e, 0, "e5m2"))
              + (mxq(f64(a_cf), 1, "e4m3") @ mxq(f64(w), 0, "e4m3")))
    return coarse + f64(a_cc) + np.diag(f64(tau))

@@ -1,0 +1,276 @@
+from contextlib import ExitStack
+
+import concourse.mybir as mybir
+from concourse.masks import make_identity
+
+C, F = 1024, 2048
+FLOPS = 2 * 2 * C * C * F
+
+F32 = mybir.dt.float32
+BF16 = mybir.dt.bfloat16
+U32 = mybir.dt.uint32
+U8 = mybir.dt.uint8
+E4M3 = mybir.dt.float8_e4m3fn_x4
+E5M2 = mybir.dt.float8_e5m2_x4
+ALU = mybir.AluOpType
+
+P = 128
+PACK = 4
+K_PASS = P * PACK
+PASSES = F // K_PASS
+N = 512
+HALVES = C // N
+M_TILES = C // P
+BANKS = 8
+TURN_BANKS = 2
+ROW_BUFS = 8
+COL_BUFS = 6
+AHEAD = 8
+QUOTA = 6
+LAG = 1
+WLAG = 1
+COLS = "W00 E00 W01 E01 W02 E02 W03 E03 W10 E10 W11 E11 W12 E12 W13 E13"
+ROWS = "A0 A1 A2 A3 A4 A5 Z0 Z1 Z2 Z3 Z4 Z5 A6 Z6 A7 Z7"
+PW0 = (2, 2, 2, 2)
+PW1 = (1, 1, 1, 1)
+PE0 = (0, 0, 0, 0)
+PE1 = (0, 0, 0, 0)
+ESP = 1
+QFIRST = 1
+QEF = 1
+STB = (0, 0, 0, 0)
+Q0 = 4
+R0 = 8
+WOV = 4
+EB = 4
+Q1 = 8
+Q2 = 12
+GB = 3
+WARM = 0
+ELAG = 1
+STORE_LAG = 1
+AHEADR = 5
+VW = 4
+RLAG = 2
+STA = (0, 0, 0, 0)
+QWA = 1
+QWB = 2
+QE = 2
+RDY = 0
+ACC_AT = (11, 17)
+
+
+def tile_galerkin_coarse_operator_s2_kernel(tc, z, a_fc, d, w, a_cf, a_cc, tau, out):
+    nc = tc.nc
+    early = BANKS - TURN_BANKS
+    rows = [("A", m, 0) for m in range(early)] + [("Z", m, 0) for m in range(early)]
+    for m in range(early, M_TILES):
+        rows.extend([("A", m, 0), ("Z", m, 0)])
+    cols = [(x[0], int(x[1]), int(x[2])) for x in COLS.split()]
+    rows = [(x[0], int(x[1]), 0) for x in ROWS.split()]
+
+    with ExitStack() as ctx:
+        keep = ctx.enter_context(tc.tile_pool(name="keep", bufs=1))
+        stage = ctx.enter_context(tc.tile_pool(name="stage", bufs=1))
+        psum = ctx.enter_context(tc.psum_pool(name="psum", bufs=1))
+        ctx.enter_context(tc.manual_schedule())
+
+        ident = keep.tile([P, P], F32, name="ident")
+        make_identity(nc, ident[:])
+
+        d_sb = keep.tile([P, PASSES, PACK], BF16, name="d_sb")
+        nc.scalar.dma_start(out=d_sb[:], in_=d.rearrange("(g p j) -> p g j", p=P, j=PACK))
+        tau_sb = keep.tile([P, M_TILES, 2], BF16, name="tau_sb")
+
+        raw, mid, grouped, codes, scales, cc = {}, {}, {}, {}, {}, {}
+        count = {"row": 0, "W": 0, "E": 0, "turn": 0, "grouped": 0, "res": 0, "woven": 0}
+
+        def load(item):
+            kind, a, g = item
+            if kind in ("A", "Z"):
+                src = a_cf if kind == "A" else z
+                raw[item] = stage.tile([P, F], BF16, name="rows", tag="rows%d" % (count["row"] % ROW_BUFS))
+                count["row"] += 1
+                nc.sync.dma_start(out=raw[item][:], in_=src[a * P:(a + 1) * P, :])
+            else:
+                src = w if kind == "W" else a_fc
+                raw[item] = stage.tile([P, PACK, N], BF16, name="cols", tag="cols%s%d" % (kind, count[kind] % (COL_BUFS if kind == "W" else EB)))
+                count[kind] += 1
+                rows = src[g * K_PASS:(g + 1) * K_PASS, a * N:(a + 1) * N]
+                nc.sync.dma_start(out=raw[item][:], in_=rows.rearrange("(p j) n -> p j n", j=PACK))
+
+        def load_cc(h):
+            cc[h] = keep.tile([P, M_TILES, N], BF16, name="cc%d" % h)
+            nc.sync.dma_start(out=cc[h][:], in_=a_cc[:, h * N:(h + 1) * N].rearrange("(m p) n -> p m n", p=P))
+
+        def first(item):
+            kind, a, g = item
+            if kind in ("A", "Z"):
+                words = raw[item][:].bitcast(F32)
+                mid[item] = []
+                for b in range(PASSES // 2):
+                    bank = psum.tile([P, 2, 2, P], F32, name="turn", tag="bank%d" % (BANKS - 1 - count["turn"] % TURN_BANKS))
+                    count["turn"] += 1
+                    for i in range(2):
+                        w0 = (2 * b + i) * 2 * P
+                        for u in range(2):
+                            nc.tensor.transpose(bank[:, i, u, :], words[:, w0 + u:w0 + 2 * P:2], ident[:])
+                    if b == 0:
+                        grouped[item] = stage.tile([P, F], BF16, name="grouped", tag="grouped%d" % (count["grouped"] % GB), align_bytes=64)
+                        count["grouped"] += 1
+                    dst = grouped[item][:, b * 2 * K_PASS:(b + 1) * 2 * K_PASS].bitcast(F32)
+                    nc.scalar.copy(out=dst.rearrange("p (i r u) -> p i r u", i=2, u=2), in_=bank[:].rearrange("p i u r -> p i r u"))
+
+        def make_e(item, j):
+            kind, a, g = item
+            nc.vector.scalar_tensor_tensor(
+                out=raw[item][:, j, :], in0=raw[("W", a, g)][:, j, :], scalar=d_sb[:, g, j:j + 1],
+                in1=raw[item][:, j, :], op0=ALU.mult, op1=ALU.add)
+
+        def second(item, part, on_vector):
+            if part == 0:
+                grouped[item] = stage.tile([P, F], BF16, name="grouped", tag="woven%d" % (count["woven"] % WOV), align_bytes=64)
+                count["woven"] += 1
+            half = N // 2
+            dst = grouped[item][:, part * half * PACK:(part + 1) * half * PACK].rearrange("p (c i t) -> p c t i", i=4, t=PACK)
+            src = raw[item][:, :, part * half:(part + 1) * half].rearrange("p t (c i) -> p c t i", i=4)
+            if on_vector:
+                nc.vector.tensor_copy(out=dst, in_=src)
+            else:
+                nc.scalar.copy(out=dst, in_=src)
+
+        def third(item):
+            name = "%s%d%d" % item
+            codes[item] = keep.tile([P, N], U32, name="codes" + name, align_bytes=64)
+            scales[item] = keep.tile([P, N], U8, name="scales" + name, align_bytes=64)
+            fmt = E5M2 if item[0] == "E" else E4M3
+            nc.vector.quantize_mx(out=codes[item][:].bitcast(fmt), scales=scales[item][:], in_=grouped[item][:])
+
+        groups = [(h, m) for h in range(HALVES) for m in range(M_TILES)]
+        todo = {grp: [(s, g) for g in range(PASSES) for s in ("A", "Z")] for grp in groups}
+        acc = {}
+        bank_of = {}
+        free_banks = list(range(BANKS - TURN_BANKS))
+        finished = []
+
+        def multiply(ready, quota):
+            done = []
+            for grp in groups:
+                h, m = grp
+                for s, g in list(todo[grp]):
+                    left, right = (s, m, 0), ("W" if s == "A" else "E", h, g)
+                    if quota == 0 or left not in ready or right not in ready:
+                        continue
+                    if grp not in acc:
+                        if not free_banks:
+                            continue
+                        bank_of[grp] = free_banks.pop(0)
+                        acc[grp] = psum.tile([P, N], F32, name="acc", tag="bank%d" % bank_of[grp])
+                    start = len(todo[grp]) == 2 * PASSES
+                    todo[grp].remove((s, g))
+                    cols = slice(g * P, (g + 1) * P)
+                    nc.tensor.matmul_mx(
+                        out=acc[grp][:],
+                        lhsT=codes[left][:, cols].bitcast(E4M3), lhsT_scale=scales[left][:, cols],
+                        rhs=codes[right][:].bitcast(E4M3 if s == "A" else E5M2), rhs_scale=scales[right][:],
+                        start=start, stop=not todo[grp])
+                    quota -= 1
+                    if not todo[grp]:
+                        done.append(grp)
+            return done
+
+        def finish(grp):
+            h, m = grp
+            res = stage.tile([P, N], F32, name="res", tag="res%d" % (count["res"] % 6))
+            count["res"] += 1
+            nc.vector.tensor_tensor(out=res[:], in0=acc[grp][:], in1=cc[h][:, m, :], op=ALU.add)
+            free_banks.append(bank_of[grp])
+            return res
+
+        def store(grp, res):
+            h, m = grp
+            if m * P // N == h:
+                diag = res[:, m * P - h * N:(m + 1) * P - h * N]
+                nc.vector.scalar_tensor_tensor(out=diag, in0=ident[:], scalar=tau_sb[:, m, 0:1], in1=diag, op0=ALU.mult, op1=ALU.add)
+            nc.sync.dma_start(out=out[m * P:(m + 1) * P, h * N:(h + 1) * N], in_=res[:])
+
+        def loads(r):
+            if r < len(rows):
+                load(rows[r])
+                load(cols[r])
+            if r in ACC_AT:
+                load_cc(ACC_AT.index(r))
+            if r == AHEADR:
+                with nc.allow_non_contiguous_dma(reason="one shift for each partition"):
+                    nc.sync.dma_start(out=tau_sb[:, :, 0:1], in_=tau.rearrange("(m p o) -> p m o", p=P, o=1))
+
+        for r in range(AHEADR):
+            loads(r)
+        if WARM:
+            ones = keep.tile([P, F], BF16, name="ones", align_bytes=64)
+            nc.vector.memset(ones[:], 1.0)
+            grouped["U", 0, 0] = ones
+            third(("U", 0, 0))
+
+        def warm(count_):
+            u = ("U", 0, 0)
+            idle = psum.tile([P, N], F32, name="acc", tag="bank%d" % (BANKS - TURN_BANKS - 1))
+            for i in range(count_):
+                nc.tensor.matmul_mx(out=idle[:], lhsT=codes[u][:, 0:P].bitcast(E4M3), lhsT_scale=scales[u][:, 0:P],
+                                    rhs=codes[u][:].bitcast(E4M3), rhs_scale=scales[u][:], start=True, stop=True)
+
+        if WARM:
+            warm(6)
+        closed, summed, ready = [], [], set()
+        r = 0
+        while any(todo.values()) or closed or summed:
+            made = []
+            if r < len(rows):
+                first(rows[r])
+            for grp, res, at in [x for x in summed if x[2] + STORE_LAG == r]:
+                store(grp, res)
+            summed = [x for x in summed if x[2] + STORE_LAG > r] + [(grp, finish(grp), r) for grp in closed]
+            for q in range(len(cols)):
+                item, age = cols[q], r - q
+                h, g = item[1], item[2]
+                if item[0] == "W":
+                    if age == (0 if h == 0 else WLAG):
+                        nv = (PW0 if h == 0 else PW1)[g]
+                        second(item, 0, nv > 1)
+                        second(item, 1, nv > 0)
+                else:
+                    nv = (PE0 if h == 0 else PE1)[g]
+                    if age == ELAG:
+                        second(item, 0, nv > 1)
+                    if age == ELAG + ESP:
+                        second(item, 1, nv > 0)
+            if QFIRST and 0 <= r - RLAG < len(rows):
+                third(rows[r - RLAG])
+                made.append(rows[r - RLAG])
+            for q in range(len(cols)):
+                item, age = cols[q], r - q
+                if item[0] == "W" and age == (QWA if item[1] == 0 else QWB) or item[0] == "E" and age == ELAG + QE and QEF:
+                    third(item)
+                    made.append(item)
+                if item[0] == "E":
+                    for j in range(PACK):
+                        if age == (STA if item[1] == 0 else STB)[j]:
+                            make_e(item, j)
+            if not QFIRST and 0 <= r - RLAG < len(rows):
+                third(rows[r - RLAG])
+                made.append(rows[r - RLAG])
+            for q in range(len(cols)):
+                item, age = cols[q], r - q
+                if item[0] == "E" and age == ELAG + QE and not QEF:
+                    third(item)
+                    made.append(item)
+            if r == len(rows):
+                free_banks.extend(range(BANKS - TURN_BANKS, BANKS))
+            if r < WARM:
+                warm(2)
+            if RDY:
+                ready = ready | set(made)
+            closed = multiply(ready, Q0 if r < R0 else Q1 if r < len(rows) else Q2)
+            ready = ready | set(made)
+            loads(r + AHEADR)
+            r += 1

@@ -23,7 +23,7 @@ HALVES = C // N
 M_TILES = C // P
 BANKS = 8
 TURN_BANKS = 2
-ROW_BUFS = 8
+ROW_BUFS = 7
 COL_BUFS = 6
 AHEAD = 8
 QUOTA = 6
@@ -32,32 +32,39 @@ WLAG = 1
 COLS = "W00 E00 W01 E01 W02 E02 W03 E03 W10 E10 W11 E11 W12 E12 W13 E13"
 ROWS = "A0 A1 A2 A3 A4 A5 Z0 Z1 Z2 Z3 Z4 Z5 A6 Z6 A7 Z7"
 PW0 = (2, 2, 2, 2)
-PW1 = (1, 1, 1, 1)
+PW1 = (0, 0, 0, 0)
 PE0 = (0, 0, 0, 0)
-PE1 = (0, 0, 0, 0)
-ESP = 1
+PE1 = (0, 0, 0, 1)
+ESP = 0
+Q3 = 2
+CAT = 0
+BEGIN = (0, 1, 2, 3, 5, 6, 7, 8, 10, 10, 13, 13, 16, 16, 19, 19)
+QS = (8, 8, 8, 8, 8, 8, 8, 8, 8, 8, 8, 8, 8, 8, 8, 8)
+MINQ = 3
+W0 = 4
+SORT = (0, 0, 0, 0, 0, 0, 0, 0, 0, 0, 0, 0, 0, 0, 0, 0)
 QFIRST = 1
-QEF = 1
-STB = (0, 0, 0, 0)
+QEF = 0
+STB = (0, 0, 1, 1)
 Q0 = 4
-R0 = 8
+R0 = 4
 WOV = 4
 EB = 4
-Q1 = 8
-Q2 = 12
+Q1 = 4
+Q2 = 6
 GB = 3
-WARM = 0
-ELAG = 1
+WARM = 5
+ELAG = 2
 STORE_LAG = 1
-AHEADR = 5
+AHEADR = 4
 VW = 4
-RLAG = 2
+RLAG = 1
 STA = (0, 0, 0, 0)
-QWA = 1
+QWA = 0
 QWB = 2
-QE = 2
+QE = 1
 RDY = 0
-ACC_AT = (11, 17)
+ACC_AT = (13, 17)
 
 
 def tile_galerkin_coarse_operator_s2_kernel(tc, z, a_fc, d, w, a_cf, a_cc, tau, out):
@@ -78,12 +85,29 @@ def tile_galerkin_coarse_operator_s2_kernel(tc, z, a_fc, d, w, a_cf, a_cc, tau, 
         ident = keep.tile([P, P], F32, name="ident")
         make_identity(nc, ident[:])
 
+        small = keep.tile([P, 3 * P], F32, name="small")
+        tau_rows = keep.tile([M_TILES, P], BF16, name="tau_rows")
+        d_rows = keep.tile([PASSES, K_PASS], BF16, name="d_rows")
+        nc.vector.memset(small[:], 0.0)
+        nc.scalar.dma_start(out=d_rows[:], in_=d.rearrange("(g k) -> g k", g=PASSES))
+        nc.scalar.dma_start(out=tau_rows[:], in_=tau.rearrange("(m p) -> m p", p=P))
         d_sb = keep.tile([P, PASSES, PACK], BF16, name="d_sb")
-        nc.scalar.dma_start(out=d_sb[:], in_=d.rearrange("(g p j) -> p g j", p=P, j=PACK))
-        tau_sb = keep.tile([P, M_TILES, 2], BF16, name="tau_sb")
+        tau_sb = keep.tile([P, M_TILES], F32, name="tau_sb")
+
+        def constants():
+            nc.vector.tensor_copy(out=small[0:PASSES, 0:2 * P], in_=d_rows[:].bitcast(F32))
+            nc.vector.tensor_copy(out=small[0:M_TILES, 2 * P:3 * P], in_=tau_rows[:])
+            bank = psum.tile([P, 3, P], F32, name="turn", tag="bank%d" % (BANKS - TURN_BANKS - 2))
+            for u in range(2):
+                nc.tensor.transpose(bank[:, u, :], small[:, u:2 * P:2], ident[:])
+            nc.tensor.transpose(bank[:, 2, :], small[:, 2 * P:3 * P], ident[:])
+            nc.scalar.copy(out=d_sb[:].rearrange("p g j -> p (g j)").bitcast(F32).rearrange("p (g u) -> p g u", u=2),
+                           in_=bank[:, 0:2, 0:PASSES].rearrange("p u g -> p g u"))
+            nc.scalar.copy(out=tau_sb[:], in_=bank[:, 2, 0:M_TILES])
 
         raw, mid, grouped, codes, scales, cc = {}, {}, {}, {}, {}, {}
-        count = {"row": 0, "W": 0, "E": 0, "turn": 0, "grouped": 0, "res": 0, "woven": 0}
+        count = {"row": 0, "W": 0, "E": 0, "turn": 0, "grouped": 0, "res": 0, "woven": 0, "sorted": 0, "mm": 0}
+        sorted_ = {}
 
         def load(item):
             kind, a, g = item
@@ -96,17 +120,18 @@ def tile_galerkin_coarse_operator_s2_kernel(tc, z, a_fc, d, w, a_cf, a_cc, tau, 
                 src = w if kind == "W" else a_fc
                 raw[item] = stage.tile([P, PACK, N], BF16, name="cols", tag="cols%s%d" % (kind, count[kind] % (COL_BUFS if kind == "W" else EB)))
                 count[kind] += 1
-                rows = src[g * K_PASS:(g + 1) * K_PASS, a * N:(a + 1) * N]
+                rows = src[g * K_PASS:(g + 1) * K_PASS, (1 - a) * N:(2 - a) * N]
                 nc.sync.dma_start(out=raw[item][:], in_=rows.rearrange("(p j) n -> p j n", j=PACK))
 
         def load_cc(h):
             cc[h] = keep.tile([P, M_TILES, N], BF16, name="cc%d" % h)
-            nc.sync.dma_start(out=cc[h][:], in_=a_cc[:, h * N:(h + 1) * N].rearrange("(m p) n -> p m n", p=P))
+            nc.sync.dma_start(out=cc[h][:], in_=a_cc[:, (1 - h) * N:(2 - h) * N].rearrange("(m p) n -> p m n", p=P))
 
         def first(item):
             kind, a, g = item
             if kind in ("A", "Z"):
-                words = raw[item][:].bitcast(F32)
+                flat = item in sorted_
+                words = sorted_[item][:] if flat else raw[item][:].bitcast(F32)
                 mid[item] = []
                 for b in range(PASSES // 2):
                     bank = psum.tile([P, 2, 2, P], F32, name="turn", tag="bank%d" % (BANKS - 1 - count["turn"] % TURN_BANKS))
@@ -114,12 +139,22 @@ def tile_galerkin_coarse_operator_s2_kernel(tc, z, a_fc, d, w, a_cf, a_cc, tau, 
                     for i in range(2):
                         w0 = (2 * b + i) * 2 * P
                         for u in range(2):
-                            nc.tensor.transpose(bank[:, i, u, :], words[:, w0 + u:w0 + 2 * P:2], ident[:])
+                            nc.tensor.transpose(bank[:, i, u, :], words[:, w0 + u * P:w0 + (u + 1) * P] if flat else words[:, w0 + u:w0 + 2 * P:2], ident[:])
                     if b == 0:
                         grouped[item] = stage.tile([P, F], BF16, name="grouped", tag="grouped%d" % (count["grouped"] % GB), align_bytes=64)
                         count["grouped"] += 1
                     dst = grouped[item][:, b * 2 * K_PASS:(b + 1) * 2 * K_PASS].bitcast(F32)
                     nc.scalar.copy(out=dst.rearrange("p (i r u) -> p i r u", i=2, u=2), in_=bank[:].rearrange("p i u r -> p i r u"))
+
+        def sort(item, on_vector):
+            sorted_[item] = stage.tile([P, F // 2], F32, name="sorted", tag="sorted%d" % (count["sorted"] % 2))
+            count["sorted"] += 1
+            dst = sorted_[item][:].rearrange("p (g u c) -> p g u c", g=PASSES, u=2)
+            src = raw[item][:].bitcast(F32).rearrange("p (g c u) -> p g u c", g=PASSES, u=2)
+            if on_vector:
+                nc.vector.tensor_copy(out=dst, in_=src)
+            else:
+                nc.scalar.copy(out=dst, in_=src)
 
         def make_e(item, j):
             kind, a, g = item
@@ -175,6 +210,7 @@ def tile_galerkin_coarse_operator_s2_kernel(tc, z, a_fc, d, w, a_cf, a_cc, tau, 
                         rhs=codes[right][:].bitcast(E4M3 if s == "A" else E5M2), rhs_scale=scales[right][:],
                         start=start, stop=not todo[grp])
                     quota -= 1
+                    count["mm"] += 1
                     if not todo[grp]:
                         done.append(grp)
             return done
@@ -183,32 +219,38 @@ def tile_galerkin_coarse_operator_s2_kernel(tc, z, a_fc, d, w, a_cf, a_cc, tau, 
             h, m = grp
             res = stage.tile([P, N], F32, name="res", tag="res%d" % (count["res"] % 6))
             count["res"] += 1
-            nc.vector.tensor_tensor(out=res[:], in0=acc[grp][:], in1=cc[h][:, m, :], op=ALU.add)
+            parts = 2 if grp == groups[-1] else 1
+            for i in range(parts):
+                c = slice(i * N // parts, (i + 1) * N // parts)
+                nc.vector.tensor_tensor(out=res[:, c], in0=acc[grp][:, c], in1=cc[h][:, m, c], op=ALU.add)
             free_banks.append(bank_of[grp])
             return res
 
         def store(grp, res):
             h, m = grp
-            if m * P // N == h:
-                diag = res[:, m * P - h * N:(m + 1) * P - h * N]
-                nc.vector.scalar_tensor_tensor(out=diag, in0=ident[:], scalar=tau_sb[:, m, 0:1], in1=diag, op0=ALU.mult, op1=ALU.add)
-            nc.sync.dma_start(out=out[m * P:(m + 1) * P, h * N:(h + 1) * N], in_=res[:])
+            n0 = (1 - h) * N
+            if n0 <= m * P < n0 + N:
+                diag = res[:, m * P - n0:(m + 1) * P - n0]
+                nc.vector.scalar_tensor_tensor(out=diag, in0=ident[:], scalar=tau_sb[:, m:m + 1], in1=diag, op0=ALU.mult, op1=ALU.add)
+            parts = 2 if grp == groups[-1] else 1
+            for i in range(parts):
+                c0, c1 = i * N // parts, (i + 1) * N // parts
+                nc.sync.dma_start(out=out[m * P:(m + 1) * P, n0 + c0:n0 + c1], in_=res[:, c0:c1])
 
         def loads(r):
             if r < len(rows):
                 load(rows[r])
-                load(cols[r])
+            for q in range(len(cols)):
+                if BEGIN[q] == r:
+                    load(cols[q])
             if r in ACC_AT:
                 load_cc(ACC_AT.index(r))
-            if r == AHEADR:
-                with nc.allow_non_contiguous_dma(reason="one shift for each partition"):
-                    nc.sync.dma_start(out=tau_sb[:, :, 0:1], in_=tau.rearrange("(m p o) -> p m o", p=P, o=1))
 
         for r in range(AHEADR):
             loads(r)
         if WARM:
-            ones = keep.tile([P, F], BF16, name="ones", align_bytes=64)
-            nc.vector.memset(ones[:], 1.0)
+            ones = stage.tile([P, F], BF16, name="ones", tag="woven3", align_bytes=64)
+            nc.vector.memset(ones[:].bitcast(U32), 0)
             grouped["U", 0, 0] = ones
             third(("U", 0, 0))
 
@@ -220,18 +262,26 @@ def tile_galerkin_coarse_operator_s2_kernel(tc, z, a_fc, d, w, a_cf, a_cc, tau, 
                                     rhs=codes[u][:].bitcast(E4M3), rhs_scale=scales[u][:], start=True, stop=True)
 
         if WARM:
-            warm(6)
+            warm(W0)
+        if CAT == 0:
+            constants()
         closed, summed, ready = [], [], set()
         r = 0
         while any(todo.values()) or closed or summed:
             made = []
             if r < len(rows):
                 first(rows[r])
+            if r == 0 and CAT == 1:
+                constants()
+            if r + 1 < len(rows) and SORT[r + 1] == 1:
+                sort(rows[r + 1], False)
+            if r + 1 < len(rows) and SORT[r + 1] == 2:
+                sort(rows[r + 1], True)
             for grp, res, at in [x for x in summed if x[2] + STORE_LAG == r]:
                 store(grp, res)
             summed = [x for x in summed if x[2] + STORE_LAG > r] + [(grp, finish(grp), r) for grp in closed]
             for q in range(len(cols)):
-                item, age = cols[q], r - q
+                item, age = cols[q], r - BEGIN[q]
                 h, g = item[1], item[2]
                 if item[0] == "W":
                     if age == (0 if h == 0 else WLAG):
@@ -248,7 +298,7 @@ def tile_galerkin_coarse_operator_s2_kernel(tc, z, a_fc, d, w, a_cf, a_cc, tau, 
                 third(rows[r - RLAG])
                 made.append(rows[r - RLAG])
             for q in range(len(cols)):
-                item, age = cols[q], r - q
+                item, age = cols[q], r - BEGIN[q]
                 if item[0] == "W" and age == (QWA if item[1] == 0 else QWB) or item[0] == "E" and age == ELAG + QE and QEF:
                     third(item)
                     made.append(item)
@@ -260,17 +310,18 @@ def tile_galerkin_coarse_operator_s2_kernel(tc, z, a_fc, d, w, a_cf, a_cc, tau, 
                 third(rows[r - RLAG])
                 made.append(rows[r - RLAG])
             for q in range(len(cols)):
-                item, age = cols[q], r - q
+                item, age = cols[q], r - BEGIN[q]
                 if item[0] == "E" and age == ELAG + QE and not QEF:
                     third(item)
                     made.append(item)
             if r == len(rows):
                 free_banks.extend(range(BANKS - TURN_BANKS, BANKS))
-            if r < WARM:
-                warm(2)
             if RDY:
                 ready = ready | set(made)
-            closed = multiply(ready, Q0 if r < R0 else Q1 if r < len(rows) else Q2)
+            closed = multiply(ready, QS[r] if r < len(rows) else Q2 if len(ready) < len(rows) + len(cols) else Q3)
+            if r < WARM and count["mm"] < MINQ:
+                warm(MINQ - count["mm"])
+            count["mm"] = 0
             ready = ready | set(made)
             loads(r + AHEADR)
             r += 1

@@ -22,7 +22,7 @@ N = 512
 HALVES = C // N
 M_TILES = C // P
 BANKS = 8
-TURN_BANKS = 2
+TURN_BANKS = 3
 ROW_BUFS = 7
 COL_BUFS = 6
 AHEAD = 8
@@ -30,41 +30,51 @@ QUOTA = 6
 LAG = 1
 WLAG = 1
 COLS = "W00 E00 W01 E01 W02 E02 W03 E03 W10 E10 W11 E11 W12 E12 W13 E13"
-ROWS = "A0 A1 A2 A3 A4 A5 Z0 Z1 Z2 Z3 Z4 Z5 A6 Z6 A7 Z7"
+ROWS = "A0 A1 A2 Z0 A3 Z1 A4 Z2 A5 Z3 A6 Z4 A7 Z5 Z6 Z7"
 PW0 = (2, 2, 2, 2)
-PW1 = (0, 0, 0, 0)
+PW1 = (2, 0, 0, 0)
 PE0 = (0, 0, 0, 0)
 PE1 = (0, 0, 0, 1)
-ESP = 0
+ESP = 1
+ELAG1 = 2
+ESP1 = 0
+QE1 = 1
+QEF1 = 1
+WSP = 0
+CUT = 512
+XV = 1
+SPLIT0 = 0
+COLFIRST = 0
+W1 = 0
 Q3 = 2
 CAT = 0
-BEGIN = (0, 1, 2, 3, 5, 6, 7, 8, 10, 10, 13, 13, 16, 16, 19, 19)
-QS = (8, 8, 8, 8, 8, 8, 8, 8, 8, 8, 8, 8, 8, 8, 8, 8)
-MINQ = 3
-W0 = 4
+BEGIN = (0, 1, 3, 4, 6, 7, 9, 10, 14, 14, 18, 18, 20, 20, 22, 22)
+QS = (3, 3, 3, 3, 3, 3, 3, 3, 3, 3, 3, 3, 3, 3, 3, 3)
+MINQ = 2
+W0 = 2
 SORT = (0, 0, 0, 0, 0, 0, 0, 0, 0, 0, 0, 0, 0, 0, 0, 0)
-QFIRST = 1
-QEF = 0
-STB = (0, 0, 1, 1)
+QFIRST = 0
+QEF = 1
+STB = (0, 0, 0, 1)
 Q0 = 4
 R0 = 4
 WOV = 4
 EB = 4
 Q1 = 4
-Q2 = 6
+Q2 = 7
 GB = 3
 WARM = 5
 ELAG = 2
 STORE_LAG = 1
-AHEADR = 4
+AHEADR = 3
 VW = 4
 RLAG = 1
-STA = (0, 0, 0, 0)
-QWA = 0
-QWB = 2
-QE = 1
+STA = (0, 0, 1, 1)
+QWA = 1
+QWB = 3
+QE = 3
 RDY = 0
-ACC_AT = (13, 17)
+ACC_AT = (15, 23)
 
 
 def tile_galerkin_coarse_operator_s2_kernel(tc, z, a_fc, d, w, a_cf, a_cc, tau, out):
@@ -121,7 +131,10 @@ def tile_galerkin_coarse_operator_s2_kernel(tc, z, a_fc, d, w, a_cf, a_cc, tau, 
                 raw[item] = stage.tile([P, PACK, N], BF16, name="cols", tag="cols%s%d" % (kind, count[kind] % (COL_BUFS if kind == "W" else EB)))
                 count[kind] += 1
                 rows = src[g * K_PASS:(g + 1) * K_PASS, (1 - a) * N:(2 - a) * N]
-                nc.sync.dma_start(out=raw[item][:], in_=rows.rearrange("(p j) n -> p j n", j=PACK))
+                parts = 2 if item == cols[0] and SPLIT0 else 1
+                for i in range(parts):
+                    c = slice(i * N // parts, (i + 1) * N // parts)
+                    nc.sync.dma_start(out=raw[item][:, :, c], in_=rows[:, c].rearrange("(p j) n -> p j n", j=PACK))
 
         def load_cc(h):
             cc[h] = keep.tile([P, M_TILES, N], BF16, name="cc%d" % h)
@@ -162,13 +175,15 @@ def tile_galerkin_coarse_operator_s2_kernel(tc, z, a_fc, d, w, a_cf, a_cc, tau, 
                 out=raw[item][:, j, :], in0=raw[("W", a, g)][:, j, :], scalar=d_sb[:, g, j:j + 1],
                 in1=raw[item][:, j, :], op0=ALU.mult, op1=ALU.add)
 
-        def second(item, part, on_vector):
+        def second(item, part, on_vector, cut=N // 2):
             if part == 0:
                 grouped[item] = stage.tile([P, F], BF16, name="grouped", tag="woven%d" % (count["woven"] % WOV), align_bytes=64)
                 count["woven"] += 1
-            half = N // 2
-            dst = grouped[item][:, part * half * PACK:(part + 1) * half * PACK].rearrange("p (c i t) -> p c t i", i=4, t=PACK)
-            src = raw[item][:, :, part * half:(part + 1) * half].rearrange("p t (c i) -> p c t i", i=4)
+            lo, hi = (0, cut) if part == 0 else (cut, N)
+            if lo == hi:
+                return
+            dst = grouped[item][:, lo * PACK:hi * PACK].rearrange("p (c i t) -> p c t i", i=4, t=PACK)
+            src = raw[item][:, :, lo:hi].rearrange("p t (c i) -> p c t i", i=4)
             if on_vector:
                 nc.vector.tensor_copy(out=dst, in_=src)
             else:
@@ -238,11 +253,13 @@ def tile_galerkin_coarse_operator_s2_kernel(tc, z, a_fc, d, w, a_cf, a_cc, tau, 
                 nc.sync.dma_start(out=out[m * P:(m + 1) * P, n0 + c0:n0 + c1], in_=res[:, c0:c1])
 
         def loads(r):
-            if r < len(rows):
+            if r < len(rows) and r >= COLFIRST:
                 load(rows[r])
             for q in range(len(cols)):
                 if BEGIN[q] == r:
                     load(cols[q])
+            if r < COLFIRST:
+                load(rows[r])
             if r in ACC_AT:
                 load_cc(ACC_AT.index(r))
 
@@ -265,6 +282,8 @@ def tile_galerkin_coarse_operator_s2_kernel(tc, z, a_fc, d, w, a_cf, a_cc, tau, 
             warm(W0)
         if CAT == 0:
             constants()
+        if W1:
+            warm(W1)
         closed, summed, ready = [], [], set()
         r = 0
         while any(todo.values()) or closed or summed:
@@ -283,23 +302,28 @@ def tile_galerkin_coarse_operator_s2_kernel(tc, z, a_fc, d, w, a_cf, a_cc, tau, 
             for q in range(len(cols)):
                 item, age = cols[q], r - BEGIN[q]
                 h, g = item[1], item[2]
-                if item[0] == "W":
-                    if age == (0 if h == 0 else WLAG):
-                        nv = (PW0 if h == 0 else PW1)[g]
-                        second(item, 0, nv > 1)
-                        second(item, 1, nv > 0)
+                if item[0] == "W" and (h == 0 or g < XV):
+                    if age == 0:
+                        cut = N // 2 if q == 0 else CUT
+                        second(item, 0, True, cut)
+                        second(item, 1, q == 0, cut)
+                elif item[0] == "W":
+                    if age == WLAG:
+                        second(item, 0, False)
+                    if age == WLAG + WSP:
+                        second(item, 1, False)
                 else:
                     nv = (PE0 if h == 0 else PE1)[g]
-                    if age == ELAG:
+                    if age == (ELAG, ELAG1)[h]:
                         second(item, 0, nv > 1)
-                    if age == ELAG + ESP:
+                    if age == (ELAG + ESP, ELAG1 + ESP1)[h]:
                         second(item, 1, nv > 0)
             if QFIRST and 0 <= r - RLAG < len(rows):
                 third(rows[r - RLAG])
                 made.append(rows[r - RLAG])
             for q in range(len(cols)):
                 item, age = cols[q], r - BEGIN[q]
-                if item[0] == "W" and age == (QWA if item[1] == 0 else QWB) or item[0] == "E" and age == ELAG + QE and QEF:
+                if item[0] == "W" and age == (QWA if item[1] == 0 else QWB) or item[0] == "E" and age == (ELAG + QE, ELAG1 + QE1)[item[1]] and (QEF, QEF1)[item[1]]:
                     third(item)
                     made.append(item)
                 if item[0] == "E":
@@ -311,7 +335,7 @@ def tile_galerkin_coarse_operator_s2_kernel(tc, z, a_fc, d, w, a_cf, a_cc, tau, 
                 made.append(rows[r - RLAG])
             for q in range(len(cols)):
                 item, age = cols[q], r - BEGIN[q]
-                if item[0] == "E" and age == ELAG + QE and not QEF:
+                if item[0] == "E" and age == (ELAG + QE, ELAG1 + QE1)[item[1]] and not (QEF, QEF1)[item[1]]:
                     third(item)
                     made.append(item)
             if r == len(rows):

from contextlib import ExitStack

import concourse.mybir as mybir
from concourse.masks import make_identity

C, F = 1024, 2048
FLOPS = 2 * 2 * C * C * F

F32 = mybir.dt.float32
BF16 = mybir.dt.bfloat16
U32 = mybir.dt.uint32
U8 = mybir.dt.uint8
E4M3 = mybir.dt.float8_e4m3fn_x4
E5M2 = mybir.dt.float8_e5m2_x4
ALU = mybir.AluOpType

P = 128
PACK = 4
K_PASS = P * PACK
PASSES = F // K_PASS
N = 512
HALVES = C // N
M_TILES = C // P
BANKS = 8
TURN_BANKS = 3
ROW_BUFS = 7
COL_BUFS = 6
AHEAD = 8
QUOTA = 6
LAG = 1
WLAG = 1
COLS = "W00 E00 W01 E01 W02 E02 W03 E03 W10 E10 W11 E11 W12 E12 W13 E13"
ROWS = "A0 A1 A2 Z0 A3 Z1 A4 Z2 A5 Z3 A6 Z4 A7 Z5 Z6 Z7"
PW0 = (2, 2, 2, 2)
PW1 = (2, 0, 0, 0)
PE0 = (0, 0, 0, 0)
PE1 = (0, 0, 0, 1)
ESP = 1
ELAG1 = 2
ESP1 = 0
QE1 = 1
QEF1 = 1
WSP = 0
CUT = 512
XV = 1
SPLIT0 = 0
COLFIRST = 0
W1 = 0
Q3 = 2
CAT = 0
BEGIN = (0, 1, 3, 4, 6, 7, 9, 10, 14, 14, 18, 18, 20, 20, 22, 22)
QS = (3, 3, 3, 3, 3, 3, 3, 3, 3, 3, 3, 3, 3, 3, 3, 3)
MINQ = 2
W0 = 2
SORT = (0, 0, 0, 0, 0, 0, 0, 0, 0, 0, 0, 0, 0, 0, 0, 0)
QFIRST = 0
QEF = 1
STB = (0, 0, 0, 1)
Q0 = 4
R0 = 4
WOV = 4
EB = 4
Q1 = 4
Q2 = 7
GB = 3
WARM = 5
ELAG = 2
STORE_LAG = 1
AHEADR = 3
VW = 4
RLAG = 1
STA = (0, 0, 1, 1)
QWA = 1
QWB = 3
QE = 3
RDY = 0
ACC_AT = (15, 23)


def tile_galerkin_coarse_operator_s2_kernel(tc, z, a_fc, d, w, a_cf, a_cc, tau, out):
    nc = tc.nc
    early = BANKS - TURN_BANKS
    rows = [("A", m, 0) for m in range(early)] + [("Z", m, 0) for m in range(early)]
    for m in range(early, M_TILES):
        rows.extend([("A", m, 0), ("Z", m, 0)])
    cols = [(x[0], int(x[1]), int(x[2])) for x in COLS.split()]
    rows = [(x[0], int(x[1]), 0) for x in ROWS.split()]

    with ExitStack() as ctx:
        keep = ctx.enter_context(tc.tile_pool(name="keep", bufs=1))
        stage = ctx.enter_context(tc.tile_pool(name="stage", bufs=1))
        psum = ctx.enter_context(tc.psum_pool(name="psum", bufs=1))
        ctx.enter_context(tc.manual_schedule())

        ident = keep.tile([P, P], F32, name="ident")
        make_identity(nc, ident[:])

        small = keep.tile([P, 3 * P], F32, name="small")
        tau_rows = keep.tile([M_TILES, P], BF16, name="tau_rows")
        d_rows = keep.tile([PASSES, K_PASS], BF16, name="d_rows")
        nc.vector.memset(small[:], 0.0)
        nc.scalar.dma_start(out=d_rows[:], in_=d.rearrange("(g k) -> g k", g=PASSES))
        nc.scalar.dma_start(out=tau_rows[:], in_=tau.rearrange("(m p) -> m p", p=P))
        d_sb = keep.tile([P, PASSES, PACK], BF16, name="d_sb")
        tau_sb = keep.tile([P, M_TILES], F32, name="tau_sb")

        def constants():
            nc.vector.tensor_copy(out=small[0:PASSES, 0:2 * P], in_=d_rows[:].bitcast(F32))
            nc.vector.tensor_copy(out=small[0:M_TILES, 2 * P:3 * P], in_=tau_rows[:])
            bank = psum.tile([P, 3, P], F32, name="turn", tag="bank%d" % (BANKS - TURN_BANKS - 2))
            for u in range(2):
                nc.tensor.transpose(bank[:, u, :], small[:, u:2 * P:2], ident[:])
            nc.tensor.transpose(bank[:, 2, :], small[:, 2 * P:3 * P], ident[:])
            nc.scalar.copy(out=d_sb[:].rearrange("p g j -> p (g j)").bitcast(F32).rearrange("p (g u) -> p g u", u=2),
                           in_=bank[:, 0:2, 0:PASSES].rearrange("p u g -> p g u"))
            nc.scalar.copy(out=tau_sb[:], in_=bank[:, 2, 0:M_TILES])

        raw, mid, grouped, codes, scales, cc = {}, {}, {}, {}, {}, {}
        count = {"row": 0, "W": 0, "E": 0, "turn": 0, "grouped": 0, "res": 0, "woven": 0, "sorted": 0, "mm": 0}
        sorted_ = {}

        def load(item):
            kind, a, g = item
            if kind in ("A", "Z"):
                src = a_cf if kind == "A" else z
                raw[item] = stage.tile([P, F], BF16, name="rows", tag="rows%d" % (count["row"] % ROW_BUFS))
                count["row"] += 1
                nc.sync.dma_start(out=raw[item][:], in_=src[a * P:(a + 1) * P, :])
            else:
                src = w if kind == "W" else a_fc
                raw[item] = stage.tile([P, PACK, N], BF16, name="cols", tag="cols%s%d" % (kind, count[kind] % (COL_BUFS if kind == "W" else EB)))
                count[kind] += 1
                rows = src[g * K_PASS:(g + 1) * K_PASS, (1 - a) * N:(2 - a) * N]
                parts = 2 if item == cols[0] and SPLIT0 else 1
                for i in range(parts):
                    c = slice(i * N // parts, (i + 1) * N // parts)
                    nc.sync.dma_start(out=raw[item][:, :, c], in_=rows[:, c].rearrange("(p j) n -> p j n", j=PACK))

        def load_cc(h):
            cc[h] = keep.tile([P, M_TILES, N], BF16, name="cc%d" % h)
            nc.sync.dma_start(out=cc[h][:], in_=a_cc[:, (1 - h) * N:(2 - h) * N].rearrange("(m p) n -> p m n", p=P))

        def first(item):
            kind, a, g = item
            if kind in ("A", "Z"):
                flat = item in sorted_
                words = sorted_[item][:] if flat else raw[item][:].bitcast(F32)
                mid[item] = []
                for b in range(PASSES // 2):
                    bank = psum.tile([P, 2, 2, P], F32, name="turn", tag="bank%d" % (BANKS - 1 - count["turn"] % TURN_BANKS))
                    count["turn"] += 1
                    for i in range(2):
                        w0 = (2 * b + i) * 2 * P
                        for u in range(2):
                            nc.tensor.transpose(bank[:, i, u, :], words[:, w0 + u * P:w0 + (u + 1) * P] if flat else words[:, w0 + u:w0 + 2 * P:2], ident[:])
                    if b == 0:
                        grouped[item] = stage.tile([P, F], BF16, name="grouped", tag="grouped%d" % (count["grouped"] % GB), align_bytes=64)
                        count["grouped"] += 1
                    dst = grouped[item][:, b * 2 * K_PASS:(b + 1) * 2 * K_PASS].bitcast(F32)
                    nc.scalar.copy(out=dst.rearrange("p (i r u) -> p i r u", i=2, u=2), in_=bank[:].rearrange("p i u r -> p i r u"))

        def sort(item, on_vector):
            sorted_[item] = stage.tile([P, F // 2], F32, name="sorted", tag="sorted%d" % (count["sorted"] % 2))
            count["sorted"] += 1
            dst = sorted_[item][:].rearrange("p (g u c) -> p g u c", g=PASSES, u=2)
            src = raw[item][:].bitcast(F32).rearrange("p (g c u) -> p g u c", g=PASSES, u=2)
            if on_vector:
                nc.vector.tensor_copy(out=dst, in_=src)
            else:
                nc.scalar.copy(out=dst, in_=src)

        def make_e(item, j):
            kind, a, g = item
            nc.vector.scalar_tensor_tensor(
                out=raw[item][:, j, :], in0=raw[("W", a, g)][:, j, :], scalar=d_sb[:, g, j:j + 1],
                in1=raw[item][:, j, :], op0=ALU.mult, op1=ALU.add)

        def second(item, part, on_vector, cut=N // 2):
            if part == 0:
                grouped[item] = stage.tile([P, F], BF16, name="grouped", tag="woven%d" % (count["woven"] % WOV), align_bytes=64)
                count["woven"] += 1
            lo, hi = (0, cut) if part == 0 else (cut, N)
            if lo == hi:
                return
            dst = grouped[item][:, lo * PACK:hi * PACK].rearrange("p (c i t) -> p c t i", i=4, t=PACK)
            src = raw[item][:, :, lo:hi].rearrange("p t (c i) -> p c t i", i=4)
            if on_vector:
                nc.vector.tensor_copy(out=dst, in_=src)
            else:
                nc.scalar.copy(out=dst, in_=src)

        def third(item):
            name = "%s%d%d" % item
            codes[item] = keep.tile([P, N], U32, name="codes" + name, align_bytes=64)
            scales[item] = keep.tile([P, N], U8, name="scales" + name, align_bytes=64)
            fmt = E5M2 if item[0] == "E" else E4M3
            nc.vector.quantize_mx(out=codes[item][:].bitcast(fmt), scales=scales[item][:], in_=grouped[item][:])

        groups = [(h, m) for h in range(HALVES) for m in range(M_TILES)]
        todo = {grp: [(s, g) for g in range(PASSES) for s in ("A", "Z")] for grp in groups}
        acc = {}
        bank_of = {}
        free_banks = list(range(BANKS - TURN_BANKS))
        finished = []

        def multiply(ready, quota):
            done = []
            for grp in groups:
                h, m = grp
                for s, g in list(todo[grp]):
                    left, right = (s, m, 0), ("W" if s == "A" else "E", h, g)
                    if quota == 0 or left not in ready or right not in ready:
                        continue
                    if grp not in acc:
                        if not free_banks:
                            continue
                        bank_of[grp] = free_banks.pop(0)
                        acc[grp] = psum.tile([P, N], F32, name="acc", tag="bank%d" % bank_of[grp])
                    start = len(todo[grp]) == 2 * PASSES
                    todo[grp].remove((s, g))
                    cols = slice(g * P, (g + 1) * P)
                    nc.tensor.matmul_mx(
                        out=acc[grp][:],
                        lhsT=codes[left][:, cols].bitcast(E4M3), lhsT_scale=scales[left][:, cols],
                        rhs=codes[right][:].bitcast(E4M3 if s == "A" else E5M2), rhs_scale=scales[right][:],
                        start=start, stop=not todo[grp])
                    quota -= 1
                    count["mm"] += 1
                    if not todo[grp]:
                        done.append(grp)
            return done

        def finish(grp):
            h, m = grp
            res = stage.tile([P, N], F32, name="res", tag="res%d" % (count["res"] % 6))
            count["res"] += 1
            parts = 2 if grp == groups[-1] else 1
            for i in range(parts):
                c = slice(i * N // parts, (i + 1) * N // parts)
                nc.vector.tensor_tensor(out=res[:, c], in0=acc[grp][:, c], in1=cc[h][:, m, c], op=ALU.add)
            free_banks.append(bank_of[grp])
            return res

        def store(grp, res):
            h, m = grp
            n0 = (1 - h) * N
            if n0 <= m * P < n0 + N:
                diag = res[:, m * P - n0:(m + 1) * P - n0]
                nc.vector.scalar_tensor_tensor(out=diag, in0=ident[:], scalar=tau_sb[:, m:m + 1], in1=diag, op0=ALU.mult, op1=ALU.add)
            parts = 2 if grp == groups[-1] else 1
            for i in range(parts):
                c0, c1 = i * N // parts, (i + 1) * N // parts
                nc.sync.dma_start(out=out[m * P:(m + 1) * P, n0 + c0:n0 + c1], in_=res[:, c0:c1])

        def loads(r):
            if r < len(rows) and r >= COLFIRST:
                load(rows[r])
            for q in range(len(cols)):
                if BEGIN[q] == r:
                    load(cols[q])
            if r < COLFIRST:
                load(rows[r])
            if r in ACC_AT:
                load_cc(ACC_AT.index(r))

        for r in range(AHEADR):
            loads(r)
        if WARM:
            ones = stage.tile([P, F], BF16, name="ones", tag="woven3", align_bytes=64)
            nc.vector.memset(ones[:].bitcast(U32), 0)
            grouped["U", 0, 0] = ones
            third(("U", 0, 0))

        def warm(count_):
            u = ("U", 0, 0)
            idle = psum.tile([P, N], F32, name="acc", tag="bank%d" % (BANKS - TURN_BANKS - 1))
            for i in range(count_):
                nc.tensor.matmul_mx(out=idle[:], lhsT=codes[u][:, 0:P].bitcast(E4M3), lhsT_scale=scales[u][:, 0:P],
                                    rhs=codes[u][:].bitcast(E4M3), rhs_scale=scales[u][:], start=True, stop=True)

        if WARM:
            warm(W0)
        if CAT == 0:
            constants()
        if W1:
            warm(W1)
        closed, summed, ready = [], [], set()
        r = 0
        while any(todo.values()) or closed or summed:
            made = []
            if r < len(rows):
                first(rows[r])
            if r == 0 and CAT == 1:
                constants()
            if r + 1 < len(rows) and SORT[r + 1] == 1:
                sort(rows[r + 1], False)
            if r + 1 < len(rows) and SORT[r + 1] == 2:
                sort(rows[r + 1], True)
            for grp, res, at in [x for x in summed if x[2] + STORE_LAG == r]:
                store(grp, res)
            summed = [x for x in summed if x[2] + STORE_LAG > r] + [(grp, finish(grp), r) for grp in closed]
            for q in range(len(cols)):
                item, age = cols[q], r - BEGIN[q]
                h, g = item[1], item[2]
                if item[0] == "W" and (h == 0 or g < XV):
                    if age == 0:
                        cut = N // 2 if q == 0 else CUT
                        second(item, 0, True, cut)
                        second(item, 1, q == 0, cut)
                elif item[0] == "W":
                    if age == WLAG:
                        second(item, 0, False)
                    if age == WLAG + WSP:
                        second(item, 1, False)
                else:
                    nv = (PE0 if h == 0 else PE1)[g]
                    if age == (ELAG, ELAG1)[h]:
                        second(item, 0, nv > 1)
                    if age == (ELAG + ESP, ELAG1 + ESP1)[h]:
                        second(item, 1, nv > 0)
            if QFIRST and 0 <= r - RLAG < len(rows):
                third(rows[r - RLAG])
                made.append(rows[r - RLAG])
            for q in range(len(cols)):
                item, age = cols[q], r - BEGIN[q]
                if item[0] == "W" and age == (QWA if item[1] == 0 else QWB) or item[0] == "E" and age == (ELAG + QE, ELAG1 + QE1)[item[1]] and (QEF, QEF1)[item[1]]:
                    third(item)
                    made.append(item)
                if item[0] == "E":
                    for j in range(PACK):
                        if age == (STA if item[1] == 0 else STB)[j]:
                            make_e(item, j)
            if not QFIRST and 0 <= r - RLAG < len(rows):
                third(rows[r - RLAG])
                made.append(rows[r - RLAG])
            for q in range(len(cols)):
                item, age = cols[q], r - BEGIN[q]
                if item[0] == "E" and age == (ELAG + QE, ELAG1 + QE1)[item[1]] and not (QEF, QEF1)[item[1]]:
                    third(item)
                    made.append(item)
            if r == len(rows):
                free_banks.extend(range(BANKS - TURN_BANKS, BANKS))
            if RDY:
                ready = ready | set(made)
            closed = multiply(ready, QS[r] if r < len(rows) else Q2 if len(ready) < len(rows) + len(cols) else Q3)
            if r < WARM and count["mm"] < MINQ:
                warm(MINQ - count["mm"])
            count["mm"] = 0
            ready = ready | set(made)
            loads(r + AHEADR)
            r += 1
